import numpy as np
import ml_dtypes


def mxq(x, axis, fmt="e4m3"):
    dtype, down = {"e4m3": (ml_dtypes.float8_e4m3fn, 7), "e5m2": (ml_dtypes.float8_e5m2, 14)}[fmt]
    v = np.moveaxis(np.asarray(x, np.float32).astype(ml_dtypes.bfloat16).astype(np.float64), axis, -1)
    blocks = v.reshape(v.shape[:-1] + (-1, 32))
    amax = np.abs(blocks).max(-1, keepdims=True)
    byte = np.maximum(np.where(amax > 0, np.frexp(amax)[1] - 1 + 127, 0) - down, 1)
    scale = np.exp2(byte - 127.0)
    codes = (blocks / scale).astype(np.float32).astype(dtype).astype(np.float64)
    return np.moveaxis((codes * scale).reshape(v.shape), -1, axis)


WIDE = False


def mx_kscale(k):
    if not WIDE:
        return np.ones(k)
    levels = np.array([10, -10, 5, -5, 0])
    if k % 512:
        return np.exp2(np.random.permutation(np.resize(levels, k // 32))).repeat(32)
    a = np.empty((k // 512, 16))
    for p in range(k // 512):
        a[p, :8] = np.random.permutation(np.resize(levels, 8))
        for g in range(8):
            far = levels[np.abs(levels - a[p, g]) >= 10]
            a[p, g + 8] = far[np.random.randint(len(far))]
    return np.exp2(a.ravel()).repeat(32)


def f64(x):
    return np.asarray(x).astype(np.float64)


def striped(idx):
    return np.tile(np.asarray(idx).reshape(-1, 16).T, (8, 1)).astype(np.uint16)


def unstriped(offs):
    return offs[:16].T.reshape(-1).astype(np.int64)


def striped8(idx):
    return np.asarray(idx).reshape(8, -1, 16).transpose(0, 2, 1).reshape(128, -1).astype(np.uint16)


def unstriped8(offs):
    return offs.reshape(8, 16, -1).transpose(0, 2, 1).reshape(8, -1).astype(np.int64)


def pick8(x, idx, run):
    r = np.arange(len(x))
    return x[r[:, None], idx[r % (8 * run) // run]]


E2M1 = np.array([0.0, 0.5, 1.0, 1.5, 2.0, 3.0, 4.0, 6.0, -0.0, -0.5, -1.0, -1.5, -2.0, -3.0, -4.0, -6.0])


def pack_weight(w, fmt):
    k, n = w.shape
    w = f64(np.asarray(w, np.float32).astype(ml_dtypes.bfloat16)).reshape(k // 32, 32, n)
    amax = np.abs(w).max(1)
    if fmt == "e4m3":
        byte = np.frexp(amax)[1] - 1 + 127 - 7
    else:
        mant, ex = np.frexp(amax / 6.0)
        byte = np.where(mant > 0.5, ex, ex - 1) + 127
    byte = np.clip(np.where(amax > 0, byte, 1), 1, 254)
    scaled = (w * np.exp2(127.0 - byte)[:, None, :]).reshape(k, n).astype(np.float32)
    by_word = np.ascontiguousarray(scaled.reshape(k // 512, 128, 4, n).transpose(0, 1, 3, 2))
    if fmt == "e4m3":
        words = by_word.astype(ml_dtypes.float8_e4m3fn).view(np.uint8)
    else:
        c = by_word.astype(ml_dtypes.float4_e2m1fn).view(np.uint8) & 0xF
        words = (c[..., 0::2] | (c[..., 1::2] << 4)).reshape(k // 512, 128, 2 * n)
    return np.ascontiguousarray(words), np.ascontiguousarray(byte.astype(np.uint8).reshape(k // 512, 16, n))


def unpack_weight(words, scales, fmt):
    g, _, n = scales.shape
    words = np.ascontiguousarray(words).reshape(g, 128, n, -1)
    if fmt == "e4m3":
        vals = words.view(ml_dtypes.float8_e4m3fn).astype(np.float64)
    else:
        nib = np.empty((g, 128, n, 4), np.uint8)
        nib[..., 0::2] = words & 0xF
        nib[..., 1::2] = words >> 4
        vals = E2M1[nib]
    vals = vals * np.repeat(np.exp2(scales.astype(np.float64) - 127.0), 8, axis=1)[..., None]
    return vals.transpose(0, 1, 3, 2).reshape(g * 512, n)


K, J, R, T, U, Z, M, O, C, N, S = 512, 256, 512, 1024, 1024, 512, 1024, 128, 512, 256, 1024


def setup_inputs():
    n = np.random.standard_normal
    idx = np.stack([np.random.permutation(T)[:J] for _ in range(8)])
    idx2 = np.stack([np.random.permutation(U)[:J] for _ in range(8)])
    idx3 = np.random.permutation(M)[:J]
    idx4 = np.stack([np.random.permutation(C)[:J] for _ in range(8)])
    idx5 = np.stack([np.random.permutation(C)[:J] for _ in range(8)])
    idx6 = np.stack([np.random.permutation(J)[:O] for _ in range(8)])
    idx7 = np.stack([np.random.permutation(S)[:N] for _ in range(8)])
    fk = mx_kscale(K)
    fr = mx_kscale(R)
    fz = mx_kscale(Z)
    wp = pack_weight(n((K, R)) * 1 / np.sqrt(K) / fk[:, None] * fr, "e2m1")
    xop = pack_weight(n((Z, M)) / fz[:, None], "e2m1")
    w2p = pack_weight(n((Z, R)) * 1 / np.sqrt(Z) * fz[:, None] * fr, "e4m3")
    return {
        "ta": (np.random.randint(-7, 8, (K, T)).astype(np.float64)).astype(np.float32),
        "tb": (np.random.randint(-7, 8, (K, U)).astype(np.float64)).astype(np.float32),
        "ga": ((np.random.randint(10, 25, (K, 1)) / 64.0) * fk[:, None]).astype(np.float32),
        "gb": ((np.random.randint(4, 13, (K, 1)) / 64.0) * fk[:, None]).astype(np.float32),
        "w_words": wp[0],
        "w_scales": wp[1],
        "xo_words": xop[0],
        "xo_scales": xop[1],
        "w2_words": w2p[0],
        "w2_scales": w2p[1],
        "sa": (np.random.uniform(0.5, 1.6, (R, 1))).astype(np.float32),
        "sb": (np.random.uniform(0.5, 1.6, (R, 1))).astype(np.float32),
        "va": (np.random.randint(-7, 8, (R, S)).astype(np.float64)).astype(np.float32),
        "ea": ((np.random.randint(8, 25, (R, 1)) / 1024.0) / fr[:, None]).astype(np.float32),
        "offs": striped8(idx),
        "offs2": striped8(idx2),
        "offs3": striped(idx3),
        "offs4": striped8(idx4),
        "offs5": striped8(idx5),
        "offs6": striped8(idx6),
        "offs7": striped8(idx7),
    }


def reference(ta, tb, ga, gb, w_words, w_scales, xo_words, xo_scales, w2_words, w2_scales, sa, sb, va, ea, offs, offs2, offs3, offs4, offs5, offs6, offs7):
    idx = unstriped8(offs)
    idx2 = unstriped8(offs2)
    idx3 = unstriped(offs3)
    idx4 = unstriped8(offs4)
    idx5 = unstriped8(offs5)
    idx6 = unstriped8(offs6)
    idx7 = unstriped8(offs7)
    wu = unpack_weight(w_words, w_scales, "e2m1")
    xou = unpack_weight(xo_words, xo_scales, "e2m1")
    w2u = unpack_weight(w2_words, w2_scales, "e4m3")
    xc = pick8(f64(ta), idx, 64) * f64(ga) + pick8(f64(tb), idx2, 64) * f64(gb)
    xcq = mxq(xc, 0, "e4m3")
    a = wu.T @ xcq
    xoidx3g = xou[:, idx3]
    b = w2u.T @ xoidx3g
    pw = np.zeros((R, C))
    pw[np.arange(R)[:, None], idx4[np.arange(R) % 512 // 64]] = a
    g1 = np.maximum(pick8(pw, idx5, 64) * f64(sa), b)
    hid = pick8(g1, idx6, 64) * f64(sb)
    vc = pick8(f64(va), idx7, 64) * f64(ea)
    vcq = mxq(vc, 0, "e4m3")
    hidq = mxq(hid, 0, "e4m3")
    y = vcq.T @ hidq
    return y

@@ -1,0 +1,228 @@
+from contextlib import ExitStack
+
+import concourse.mybir as mybir
+
+K, J, R, T, U, Z, M, O, C, N, S = 512, 256, 512, 1024, 1024, 512, 1024, 128, 512, 256, 1024
+FLOPS = 2 * K * R * J + 2 * Z * R * J + 2 * R * N * O
+
+F32 = mybir.dt.float32
+BF16 = mybir.dt.bfloat16
+I32 = mybir.dt.int32
+U32 = mybir.dt.uint32
+U16 = mybir.dt.uint16
+U8 = mybir.dt.uint8
+E4M3 = mybir.dt.float8_e4m3fn_x4
+E2M1 = mybir.dt.float4_e2m1fn_x4
+COPY = mybir.ActivationFunctionType.Copy
+ADD = mybir.AluOpType.add
+MAX = mybir.AluOpType.max
+
+P = 128
+PACK = 4
+QUADS = 4
+ALIGN = 64
+
+
+def tile_picked_twobooks_plain_two_answered_codes_plain_kernel(
+    tc, ta, tb, ga, gb, w_words, w_scales, xo_words, xo_scales, w2_words, w2_scales,
+    sa, sb, va, ea, offs, offs2, offs3, offs4, offs5, offs6, offs7, out,
+):
+    nc = tc.nc
+    with ExitStack() as ctx:
+        lists = ctx.enter_context(tc.tile_pool(name="lists", bufs=1))
+        pool = ctx.enter_context(tc.tile_pool(name="pool", bufs=1))
+        psum = ctx.enter_context(tc.psum_pool(name="psum", bufs=1))
+
+        def sbuf(shape, dtype, name, tag=None):
+            return pool.tile(shape, dtype, name=name, tag=tag or name, align_bytes=ALIGN)
+
+        def load_list(source, name):
+            held = lists.tile(list(source.shape), U16, name=name)
+            nc.sync.dma_start(held[:], source)
+            return held
+
+        def load_rows(table, t, name):
+            held = sbuf([P, table.shape[1]], F32, name)
+            nc.sync.dma_start(out=held[:], in_=table.rearrange("(p t) c -> t p c", t=PACK)[t])
+            return held
+
+        def load_column(queue, column, name):
+            held = sbuf([P, PACK], F32, name)
+            queue.dma_start(out=held[:], in_=column.rearrange("(p t) o -> p (t o)", t=PACK))
+            return held
+
+        def stage_scale_rows(scales, name):
+            staged = sbuf([PACK, QUADS, scales.shape[2]], U8, name)
+            nc.sync.dma_start(
+                out=staged[:].bitcast(I32),
+                in_=scales[0].bitcast(I32).rearrange("(q i) c -> i q c", i=PACK),
+            )
+            return staged
+
+        def spread_scale_rows(staged, name):
+            plane = sbuf([P, staged.shape[2]], U8, name)
+            nc.vector.memset(plane[:].bitcast(I32), 0)
+            for q in range(QUADS):
+                nc.vector.tensor_copy(
+                    out=plane[32 * q : 32 * q + PACK, :].bitcast(I32), in_=staged[:, q, :].bitcast(I32)
+                )
+            return plane
+
+        def deal_columns(copy, dealt, source):
+            copy(out=dealt.rearrange("p (t m) -> p m t", t=PACK), in_=source.rearrange("p (m t) -> p m t", t=PACK))
+
+        def fetch_scaled(fetched, window, offsets, factor, t):
+            nc.scalar.activation(
+                out=fetched, in_=window[:].indirect(offsets[:]), func=COPY, scale=factor[:, t : t + 1]
+            )
+
+        def quantise(planes, copy, name):
+            width = planes.shape[2]
+            woven = sbuf([P, width, PACK], BF16, name + "_woven")
+            copy(
+                out=woven[:].rearrange("p (c i) t -> p c t i", i=4),
+                in_=planes[:].rearrange("p t (c i) -> p c t i", i=4),
+            )
+            return quantise_woven(woven, name)
+
+        def quantise_woven(woven, name):
+            width = woven.shape[1]
+            codes = sbuf([P, width], U32, name + "_codes")
+            plane = sbuf([P, width], U8, name + "_plane")
+            nc.vector.quantize_mx(
+                out=codes[:].bitcast(E4M3), scales=plane[:], in_=woven[:].rearrange("p c t -> p (c t)")
+            )
+            return codes, plane
+
+        xo_plane_table = sbuf([P, M], U8, "xo_plane_table")
+        nc.vector.memset(xo_plane_table[:].bitcast(I32), 0)
+        for q in range(QUADS):
+            nc.gpsimd.dma_start(
+                out=xo_plane_table[32 * q : 32 * q + PACK, :].bitcast(I32),
+                in_=xo_scales[0, PACK * q : PACK * (q + 1), :].bitcast(I32),
+            )
+        sa_sb = load_column(nc.gpsimd, sa, "sa_sb")
+        ea_sb = load_column(nc.gpsimd, ea, "ea_sb")
+        sb_sb = load_column(nc.gpsimd, sb, "sb_sb")
+
+        ta_sb = [load_rows(ta, 0, "ta0")]
+        offs_sb = load_list(offs, "offs_sb")
+        tb_sb = [load_rows(tb, 0, "tb0")]
+        ga_sb = load_column(nc.sync, ga, "ga_sb")
+        offs2_sb = load_list(offs2, "offs2_sb")
+        ta_sb.append(load_rows(ta, 1, "ta1"))
+        gb_sb = load_column(nc.sync, gb, "gb_sb")
+        w_staged = stage_scale_rows(w_scales, "w_staged")
+        tb_sb.append(load_rows(tb, 1, "tb1"))
+        w2_staged = stage_scale_rows(w2_scales, "w2_staged")
+        ta_sb.append(load_rows(ta, 2, "ta2"))
+        w_raw = sbuf([P, 2 * R], U8, "w_raw")
+        nc.sync.dma_start(out=w_raw[:].bitcast(I32), in_=w_words[0].bitcast(I32))
+        tb_sb.append(load_rows(tb, 2, "tb2"))
+        ta_sb.append(load_rows(ta, 3, "ta3"))
+        tb_sb.append(load_rows(tb, 3, "tb3"))
+        w2_raw = sbuf([P, R], U32, "w2_raw")
+        nc.sync.dma_start(out=w2_raw[:].bitcast(I32), in_=w2_words[0].rearrange("p c t -> p (c t)").bitcast(I32))
+        offs3_sb = load_list(offs3, "offs3_sb")
+        xo_table = sbuf([P, M], U16, "xo_table")
+        nc.sync.dma_start(out=xo_table[:].bitcast(I32), in_=xo_words[0].bitcast(I32))
+        offs4_sb = load_list(offs4, "offs4_sb")
+        va_sb = [load_rows(va, 0, "va0")]
+        offs7_sb = load_list(offs7, "offs7_sb")
+        offs5_sb = load_list(offs5, "offs5_sb")
+        va_sb.append(load_rows(va, 1, "va1"))
+        offs6_sb = load_list(offs6, "offs6_sb")
+        va_sb.append(load_rows(va, 2, "va2"))
+        va_sb.append(load_rows(va, 3, "va3"))
+
+        w_plane_raw = spread_scale_rows(w_staged, "w_plane_raw")
+        w2_plane_raw = spread_scale_rows(w2_staged, "w2_plane_raw")
+
+        boards = [sbuf([P, C], F32, "board%d" % t) for t in range(PACK)]
+        for board in boards:
+            nc.vector.memset(board[:], 0.0)
+
+        w_dealt = sbuf([P, 2 * R], U8, "w_dealt")
+        deal_columns(nc.scalar.copy, w_dealt[:].bitcast(U16), w_raw[:].bitcast(U16))
+        w_plane = sbuf([P, R], U8, "w_plane")
+        deal_columns(nc.vector.tensor_copy, w_plane[:], w_plane_raw[:])
+        w2_plane = sbuf([P, R], U8, "w2_plane")
+        deal_columns(nc.vector.tensor_copy, w2_plane[:], w2_plane_raw[:])
+
+        xc_woven = sbuf([P, J, PACK], BF16, "xc_woven")
+        for t in range(PACK):
+            from_ta = sbuf([P, J], F32, "from_ta%d" % t)
+            fetch_scaled(from_ta[:], ta_sb[t], offs_sb, ga_sb, t)
+            from_tb = sbuf([P, J], F32, "from_tb%d" % t)
+            fetch_scaled(from_tb[:], tb_sb[t], offs2_sb, gb_sb, t)
+            nc.vector.tensor_tensor(out=xc_woven[:, :, t], in0=from_ta[:], in1=from_tb[:], op=ADD)
+        xc_codes, xc_plane = quantise_woven(xc_woven, "xc")
+
+        w2_dealt = sbuf([P, R], U32, "w2_dealt")
+        deal_columns(nc.scalar.copy, w2_dealt[:], w2_raw[:])
+
+        a_sb = []
+        for t in range(PACK):
+            a_ps = psum.tile([P, J], F32, name="a_ps%d" % t)
+            nc.tensor.matmul_mx(
+                out=a_ps[:],
+                lhsT=w_dealt[:, 2 * P * t : 2 * P * (t + 1)].bitcast(E2M1),
+                lhsT_scale=w_plane[:, P * t : P * (t + 1)],
+                rhs=xc_codes[:].bitcast(E4M3),
+                rhs_scale=xc_plane[:],
+                start=True,
+                stop=True,
+            )
+            a_sb.append(sbuf([P, J], F32, "a_sb%d" % t))
+            nc.scalar.copy(out=a_sb[t][:], in_=a_ps[:])
+
+        xo_codes = sbuf([P, J], U16, "xo_codes")
+        nc.vector.tensor_copy(out=xo_codes[:], in_=xo_table[:].indirect(offs3_sb[:]))
+        xo_plane = sbuf([P, J], U8, "xo_plane")
+        nc.vector.tensor_copy(out=xo_plane[:], in_=xo_plane_table[:].indirect(offs3_sb[:]))
+        b_ps = [psum.tile([P, 2, J], F32, name="b_ps%d" % u) for u in range(2)]
+        for t in range(PACK):
+            nc.tensor.matmul_mx(
+                out=b_ps[t // 2][:, t % 2, :],
+                lhsT=w2_dealt[:, P * t : P * (t + 1)].bitcast(E4M3),
+                lhsT_scale=w2_plane[:, P * t : P * (t + 1)],
+                rhs=xo_codes[:].bitcast(E2M1),
+                rhs_scale=xo_plane[:],
+                start=True,
+                stop=True,
+            )
+
+        for t in range(PACK):
+            nc.vector.tensor_copy(out=boards[t][:].indirect(offs4_sb[:]), in_=a_sb[t][:])
+
+        vc_planes = sbuf([P, PACK, N], BF16, "vc_planes")
+        for t in range(PACK):
+            fetch_scaled(vc_planes[:, t, :], va_sb[t], offs7_sb, ea_sb, t)
+        vc_codes, vc_plane = quantise(vc_planes, nc.scalar.copy, "vc")
+
+        reused = ["va1", "va2", "va3", "vc_planes"]
+        g1 = []
+        for t in range(PACK):
+            read_back = sbuf([P, J], F32, "read_back%d" % t, tag=reused[t])
+            fetch_scaled(read_back[:], boards[t], offs5_sb, sa_sb, t)
+            g1.append(sbuf([P, J], F32, "g1_%d" % t))
+            nc.vector.tensor_tensor(out=g1[t][:], in0=read_back[:], in1=b_ps[t // 2][:, t % 2, :], op=MAX)
+        hid_planes = sbuf([P, PACK, O], BF16, "hid_planes", tag="board3")
+        for t in range(PACK):
+            fetch_scaled(hid_planes[:, t, :], g1[t], offs6_sb, sb_sb, t)
+        hid_codes, hid_plane = quantise(hid_planes, nc.vector.tensor_copy, "hid")
+
+        for u, (copy, queue) in enumerate(((nc.vector.tensor_copy, nc.sync), (nc.scalar.copy, nc.scalar))):
+            y_ps = psum.tile([P, O], F32, name="y_ps%d" % u)
+            nc.tensor.matmul_mx(
+                out=y_ps[:],
+                lhsT=vc_codes[:, P * u : P * (u + 1)].bitcast(E4M3),
+                lhsT_scale=vc_plane[:, P * u : P * (u + 1)],
+                rhs=hid_codes[:].bitcast(E4M3),
+                rhs_scale=hid_plane[:],
+                start=True,
+                stop=True,
+            )
+            y_sb = sbuf([P, O], F32, "y_sb%d" % u)
+            copy(out=y_sb[:], in_=y_ps[:])
+            queue.dma_start(out=out[P * u : P * (u + 1), :], in_=y_sb[:])

@@ -51,9 +51,9 @@ def tile_picked_twobooks_plain_two_answered_codes_plain_kernel(
             queue.dma_start(out=held[:], in_=column.rearrange("(p t) o -> p (t o)", t=PACK))
             return held
 
-        def stage_scale_rows(scales, name):
+        def stage_scale_rows(queue, scales, name):
             staged = sbuf([PACK, QUADS, scales.shape[2]], U8, name)
-            nc.sync.dma_start(
+            queue.dma_start(
                 out=staged[:].bitcast(I32),
                 in_=scales[0].bitcast(I32).rearrange("(q i) c -> i q c", i=PACK),
             )
@@ -62,7 +62,8 @@ def tile_picked_twobooks_plain_two_answered_codes_plain_kernel(
         def spread_scale_rows(staged, name):
             plane = sbuf([P, staged.shape[2]], U8, name)
             nc.vector.memset(plane[:].bitcast(I32), 0)
-            for q in range(QUADS):
+            nc.scalar.copy(out=plane[0:PACK, :].bitcast(U32), in_=staged[:, 0, :].bitcast(U32))
+            for q in range(1, QUADS):
                 nc.vector.tensor_copy(
                     out=plane[32 * q : 32 * q + PACK, :].bitcast(I32), in_=staged[:, q, :].bitcast(I32)
                 )
@@ -76,64 +77,64 @@ def tile_picked_twobooks_plain_two_answered_codes_plain_kernel(
                 out=fetched, in_=window[:].indirect(offsets[:]), func=COPY, scale=factor[:, t : t + 1]
             )
 
-        def quantise(planes, copy, name):
-            width = planes.shape[2]
-            woven = sbuf([P, width, PACK], BF16, name + "_woven")
-            copy(
+        def weave(planes, name, tag=None):
+            woven = sbuf([P, planes.shape[2], PACK], BF16, name, tag=tag)
+            nc.vector.tensor_copy(
                 out=woven[:].rearrange("p (c i) t -> p c t i", i=4),
-                in_=planes[:].rearrange("p t (c i) -> p c t i", i=4),
+                in_=planes.rearrange("p t (c i) -> p c t i", i=4),
             )
-            return quantise_woven(woven, name)
+            return woven
 
-        def quantise_woven(woven, name):
-            width = woven.shape[1]
-            codes = sbuf([P, width], U32, name + "_codes")
-            plane = sbuf([P, width], U8, name + "_plane")
-            nc.vector.quantize_mx(
-                out=codes[:].bitcast(E4M3), scales=plane[:], in_=woven[:].rearrange("p c t -> p (c t)")
-            )
+        def quantise(woven_halves, name):
+            half = woven_halves[0].shape[1]
+            codes = sbuf([P, 2 * half], U32, name + "_codes")
+            plane = sbuf([P, 2 * half], U8, name + "_plane")
+            for h, woven in enumerate(woven_halves):
+                nc.vector.quantize_mx(
+                    out=codes[:, half * h : half * (h + 1)].bitcast(E4M3),
+                    scales=plane[:, half * h : half * (h + 1)],
+                    in_=woven[:].rearrange("p c t -> p (c t)"),
+                )
             return codes, plane
 
         xo_plane_table = sbuf([P, M], U8, "xo_plane_table")
         nc.vector.memset(xo_plane_table[:].bitcast(I32), 0)
-        for q in range(QUADS):
-            nc.gpsimd.dma_start(
-                out=xo_plane_table[32 * q : 32 * q + PACK, :].bitcast(I32),
-                in_=xo_scales[0, PACK * q : PACK * (q + 1), :].bitcast(I32),
-            )
-        sa_sb = load_column(nc.gpsimd, sa, "sa_sb")
-        ea_sb = load_column(nc.gpsimd, ea, "ea_sb")
-        sb_sb = load_column(nc.gpsimd, sb, "sb_sb")
+
+        w_staged = stage_scale_rows(nc.scalar, w_scales, "w_staged")
+        ga_sb = load_column(nc.scalar, ga, "ga_sb")
+        gb_sb = load_column(nc.scalar, gb, "gb_sb")
 
         ta_sb = [load_rows(ta, 0, "ta0")]
         offs_sb = load_list(offs, "offs_sb")
         tb_sb = [load_rows(tb, 0, "tb0")]
-        ga_sb = load_column(nc.sync, ga, "ga_sb")
-        offs2_sb = load_list(offs2, "offs2_sb")
         ta_sb.append(load_rows(ta, 1, "ta1"))
-        gb_sb = load_column(nc.sync, gb, "gb_sb")
-        w_staged = stage_scale_rows(w_scales, "w_staged")
+        offs2_sb = load_list(offs2, "offs2_sb")
         tb_sb.append(load_rows(tb, 1, "tb1"))
-        w2_staged = stage_scale_rows(w2_scales, "w2_staged")
-        ta_sb.append(load_rows(ta, 2, "ta2"))
+        w2_staged = stage_scale_rows(nc.sync, w2_scales, "w2_staged")
+        for t in range(2, PACK):
+            ta_sb.append(load_rows(ta, t, "ta%d" % t))
+            tb_sb.append(load_rows(tb, t, "tb%d" % t))
         w_raw = sbuf([P, 2 * R], U8, "w_raw")
         nc.sync.dma_start(out=w_raw[:].bitcast(I32), in_=w_words[0].bitcast(I32))
-        tb_sb.append(load_rows(tb, 2, "tb2"))
-        ta_sb.append(load_rows(ta, 3, "ta3"))
-        tb_sb.append(load_rows(tb, 3, "tb3"))
-        w2_raw = sbuf([P, R], U32, "w2_raw")
-        nc.sync.dma_start(out=w2_raw[:].bitcast(I32), in_=w2_words[0].rearrange("p c t -> p (c t)").bitcast(I32))
+        xo_rows = xo_scales[0].bitcast(I32).rearrange("(q i) c -> i q c", i=PACK)
+        for i in range(PACK):
+            nc.sync.dma_start(out=xo_plane_table[i:P:32, :].bitcast(I32), in_=xo_rows[i])
         offs3_sb = load_list(offs3, "offs3_sb")
         xo_table = sbuf([P, M], U16, "xo_table")
         nc.sync.dma_start(out=xo_table[:].bitcast(I32), in_=xo_words[0].bitcast(I32))
         offs4_sb = load_list(offs4, "offs4_sb")
+        w2_raw = sbuf([P, R], U32, "w2_raw")
+        nc.sync.dma_start(out=w2_raw[:].bitcast(I32), in_=w2_words[0].rearrange("p c t -> p (c t)").bitcast(I32))
+        ea_sb = load_column(nc.sync, ea, "ea_sb")
         va_sb = [load_rows(va, 0, "va0")]
         offs7_sb = load_list(offs7, "offs7_sb")
         offs5_sb = load_list(offs5, "offs5_sb")
+        sa_sb = load_column(nc.sync, sa, "sa_sb")
         va_sb.append(load_rows(va, 1, "va1"))
-        offs6_sb = load_list(offs6, "offs6_sb")
         va_sb.append(load_rows(va, 2, "va2"))
         va_sb.append(load_rows(va, 3, "va3"))
+        offs6_sb = load_list(offs6, "offs6_sb")
+        sb_sb = load_column(nc.sync, sb, "sb_sb")
 
         w_plane_raw = spread_scale_rows(w_staged, "w_plane_raw")
         w2_plane_raw = spread_scale_rows(w2_staged, "w2_plane_raw")
@@ -142,24 +143,24 @@ def tile_picked_twobooks_plain_two_answered_codes_plain_kernel(
         for board in boards:
             nc.vector.memset(board[:], 0.0)
 
-        w_dealt = sbuf([P, 2 * R], U8, "w_dealt")
-        deal_columns(nc.scalar.copy, w_dealt[:].bitcast(U16), w_raw[:].bitcast(U16))
         w_plane = sbuf([P, R], U8, "w_plane")
         deal_columns(nc.vector.tensor_copy, w_plane[:], w_plane_raw[:])
         w2_plane = sbuf([P, R], U8, "w2_plane")
         deal_columns(nc.vector.tensor_copy, w2_plane[:], w2_plane_raw[:])
 
-        xc_woven = sbuf([P, J, PACK], BF16, "xc_woven")
+        xc_woven = [sbuf([P, J // 2, PACK], BF16, "xc_woven%d" % h) for h in range(2)]
         for t in range(PACK):
             from_ta = sbuf([P, J], F32, "from_ta%d" % t)
             fetch_scaled(from_ta[:], ta_sb[t], offs_sb, ga_sb, t)
             from_tb = sbuf([P, J], F32, "from_tb%d" % t)
             fetch_scaled(from_tb[:], tb_sb[t], offs2_sb, gb_sb, t)
-            nc.vector.tensor_tensor(out=xc_woven[:, :, t], in0=from_ta[:], in1=from_tb[:], op=ADD)
-        xc_codes, xc_plane = quantise_woven(xc_woven, "xc")
+            for h in range(2):
+                slots = slice(h * J // 2, (h + 1) * J // 2)
+                nc.vector.tensor_tensor(out=xc_woven[h][:, :, t], in0=from_ta[:, slots], in1=from_tb[:, slots], op=ADD)
+        xc_codes, xc_plane = quantise(xc_woven, "xc")
 
-        w2_dealt = sbuf([P, R], U32, "w2_dealt")
-        deal_columns(nc.scalar.copy, w2_dealt[:], w2_raw[:])
+        w_dealt = sbuf([P, 2 * R], U8, "w_dealt")
+        deal_columns(nc.scalar.copy, w_dealt[:].bitcast(U16), w_raw[:].bitcast(U16))
 
         a_sb = []
         for t in range(PACK):
@@ -176,10 +177,12 @@ def tile_picked_twobooks_plain_two_answered_codes_plain_kernel(
             a_sb.append(sbuf([P, J], F32, "a_sb%d" % t))
             nc.scalar.copy(out=a_sb[t][:], in_=a_ps[:])
 
+        w2_dealt = sbuf([P, R], U32, "w2_dealt")
+        deal_columns(nc.scalar.copy, w2_dealt[:], w2_raw[:])
         xo_codes = sbuf([P, J], U16, "xo_codes")
-        nc.vector.tensor_copy(out=xo_codes[:], in_=xo_table[:].indirect(offs3_sb[:]))
         xo_plane = sbuf([P, J], U8, "xo_plane")
         nc.vector.tensor_copy(out=xo_plane[:], in_=xo_plane_table[:].indirect(offs3_sb[:]))
+        nc.vector.tensor_copy(out=xo_codes[:], in_=xo_table[:].indirect(offs3_sb[:]))
         b_ps = [psum.tile([P, 2, J], F32, name="b_ps%d" % u) for u in range(2)]
         for t in range(PACK):
             nc.tensor.matmul_mx(
@@ -198,19 +201,26 @@ def tile_picked_twobooks_plain_two_answered_codes_plain_kernel(
         vc_planes = sbuf([P, PACK, N], BF16, "vc_planes")
         for t in range(PACK):
             fetch_scaled(vc_planes[:, t, :], va_sb[t], offs7_sb, ea_sb, t)
-        vc_codes, vc_plane = quantise(vc_planes, nc.scalar.copy, "vc")
 
-        reused = ["va1", "va2", "va3", "vc_planes"]
         g1 = []
         for t in range(PACK):
-            read_back = sbuf([P, J], F32, "read_back%d" % t, tag=reused[t])
+            read_back = sbuf([P, J], F32, "read_back%d" % t, tag="va%d" % t)
             fetch_scaled(read_back[:], boards[t], offs5_sb, sa_sb, t)
             g1.append(sbuf([P, J], F32, "g1_%d" % t))
             nc.vector.tensor_tensor(out=g1[t][:], in0=read_back[:], in1=b_ps[t // 2][:, t % 2, :], op=MAX)
+        vc_woven = [
+            weave(vc_planes[:, :, h * N // 2 : (h + 1) * N // 2], "vc_woven%d" % h, tag="va%d" % (2 + h))
+            for h in range(2)
+        ]
+        vc_codes, vc_plane = quantise(vc_woven, "vc")
         hid_planes = sbuf([P, PACK, O], BF16, "hid_planes", tag="board3")
         for t in range(PACK):
             fetch_scaled(hid_planes[:, t, :], g1[t], offs6_sb, sb_sb, t)
-        hid_codes, hid_plane = quantise(hid_planes, nc.vector.tensor_copy, "hid")
+        hid_woven = [
+            weave(hid_planes[:, :, h * O // 2 : (h + 1) * O // 2], "hid_woven%d" % h)
+            for h in range(2)
+        ]
+        hid_codes, hid_plane = quantise(hid_woven, "hid")
 
         for u, (copy, queue) in enumerate(((nc.vector.tensor_copy, nc.sync), (nc.scalar.copy, nc.scalar))):
             y_ps = psum.tile([P, O], F32, name="y_ps%d" % u)

@@ -103,15 +103,12 @@ def tile_picked_twobooks_plain_two_answered_codes_plain_kernel(
         w_staged = stage_scale_rows(nc.scalar, w_scales, "w_staged")
         ga_sb = load_column(nc.scalar, ga, "ga_sb")
         gb_sb = load_column(nc.scalar, gb, "gb_sb")
+        w2_staged = stage_scale_rows(nc.scalar, w2_scales, "w2_staged")
 
-        ta_sb = [load_rows(ta, 0, "ta0")]
         offs_sb = load_list(offs, "offs_sb")
-        tb_sb = [load_rows(tb, 0, "tb0")]
-        ta_sb.append(load_rows(ta, 1, "ta1"))
         offs2_sb = load_list(offs2, "offs2_sb")
-        tb_sb.append(load_rows(tb, 1, "tb1"))
-        w2_staged = stage_scale_rows(nc.sync, w2_scales, "w2_staged")
-        for t in range(2, PACK):
+        ta_sb, tb_sb = [], []
+        for t in range(PACK):
             ta_sb.append(load_rows(ta, t, "ta%d" % t))
             tb_sb.append(load_rows(tb, t, "tb%d" % t))
         w_raw = sbuf([P, 2 * R], U8, "w_raw")

@@ -113,12 +113,12 @@ def tile_picked_twobooks_plain_two_answered_codes_plain_kernel(
             tb_sb.append(load_rows(tb, t, "tb%d" % t))
         w_raw = sbuf([P, 2 * R], U8, "w_raw")
         nc.sync.dma_start(out=w_raw[:].bitcast(I32), in_=w_words[0].bitcast(I32))
-        xo_rows = xo_scales[0].bitcast(I32).rearrange("(q i) c -> i q c", i=PACK)
-        for i in range(PACK):
-            nc.sync.dma_start(out=xo_plane_table[i:P:32, :].bitcast(I32), in_=xo_rows[i])
         offs3_sb = load_list(offs3, "offs3_sb")
         xo_table = sbuf([P, M], U16, "xo_table")
         nc.sync.dma_start(out=xo_table[:].bitcast(I32), in_=xo_words[0].bitcast(I32))
+        xo_rows = xo_scales[0].bitcast(I32).rearrange("(q i) c -> i q c", i=PACK)
+        for i in range(PACK):
+            nc.sync.dma_start(out=xo_plane_table[i:P:32, :].bitcast(I32), in_=xo_rows[i])
         offs4_sb = load_list(offs4, "offs4_sb")
         w2_raw = sbuf([P, R], U32, "w2_raw")
         nc.sync.dma_start(out=w2_raw[:].bitcast(I32), in_=w2_words[0].rearrange("p c t -> p (c t)").bitcast(I32))
@@ -177,9 +177,9 @@ def tile_picked_twobooks_plain_two_answered_codes_plain_kernel(
         w2_dealt = sbuf([P, R], U32, "w2_dealt")
         deal_columns(nc.scalar.copy, w2_dealt[:], w2_raw[:])
         xo_codes = sbuf([P, J], U16, "xo_codes")
+        nc.vector.tensor_copy(out=xo_codes[:], in_=xo_table[:].indirect(offs3_sb[:]))
         xo_plane = sbuf([P, J], U8, "xo_plane")
         nc.vector.tensor_copy(out=xo_plane[:], in_=xo_plane_table[:].indirect(offs3_sb[:]))
-        nc.vector.tensor_copy(out=xo_codes[:], in_=xo_table[:].indirect(offs3_sb[:]))
         b_ps = [psum.tile([P, 2, J], F32, name="b_ps%d" % u) for u in range(2)]
         for t in range(PACK):
             nc.tensor.matmul_mx(

from contextlib import ExitStack

import concourse.mybir as mybir

K, J, R, T, U, Z, M, O, C, N, S = 512, 256, 512, 1024, 1024, 512, 1024, 128, 512, 256, 1024
FLOPS = 2 * K * R * J + 2 * Z * R * J + 2 * R * N * O

F32 = mybir.dt.float32
BF16 = mybir.dt.bfloat16
I32 = mybir.dt.int32
U32 = mybir.dt.uint32
U16 = mybir.dt.uint16
U8 = mybir.dt.uint8
E4M3 = mybir.dt.float8_e4m3fn_x4
E2M1 = mybir.dt.float4_e2m1fn_x4
COPY = mybir.ActivationFunctionType.Copy
ADD = mybir.AluOpType.add
MAX = mybir.AluOpType.max

P = 128
PACK = 4
QUADS = 4
ALIGN = 64


def tile_picked_twobooks_plain_two_answered_codes_plain_kernel(
    tc, ta, tb, ga, gb, w_words, w_scales, xo_words, xo_scales, w2_words, w2_scales,
    sa, sb, va, ea, offs, offs2, offs3, offs4, offs5, offs6, offs7, out,
):
    nc = tc.nc
    with ExitStack() as ctx:
        lists = ctx.enter_context(tc.tile_pool(name="lists", bufs=1))
        pool = ctx.enter_context(tc.tile_pool(name="pool", bufs=1))
        psum = ctx.enter_context(tc.psum_pool(name="psum", bufs=1))

        def sbuf(shape, dtype, name, tag=None):
            return pool.tile(shape, dtype, name=name, tag=tag or name, align_bytes=ALIGN)

        def load_list(source, name):
            held = lists.tile(list(source.shape), U16, name=name)
            nc.sync.dma_start(held[:], source)
            return held

        def load_rows(table, t, name):
            held = sbuf([P, table.shape[1]], F32, name)
            nc.sync.dma_start(out=held[:], in_=table.rearrange("(p t) c -> t p c", t=PACK)[t])
            return held

        def load_column(queue, column, name):
            held = sbuf([P, PACK], F32, name)
            queue.dma_start(out=held[:], in_=column.rearrange("(p t) o -> p (t o)", t=PACK))
            return held

        def stage_scale_rows(queue, scales, name):
            staged = sbuf([PACK, QUADS, scales.shape[2]], U8, name)
            queue.dma_start(
                out=staged[:].bitcast(I32),
                in_=scales[0].bitcast(I32).rearrange("(q i) c -> i q c", i=PACK),
            )
            return staged

        def spread_scale_rows(staged, name):
            plane = sbuf([P, staged.shape[2]], U8, name)
            nc.vector.memset(plane[:].bitcast(I32), 0)
            nc.scalar.copy(out=plane[0:PACK, :].bitcast(U32), in_=staged[:, 0, :].bitcast(U32))
            for q in range(1, QUADS):
                nc.vector.tensor_copy(
                    out=plane[32 * q : 32 * q + PACK, :].bitcast(I32), in_=staged[:, q, :].bitcast(I32)
                )
            return plane

        def deal_columns(copy, dealt, source):
            copy(out=dealt.rearrange("p (t m) -> p m t", t=PACK), in_=source.rearrange("p (m t) -> p m t", t=PACK))

        def fetch_scaled(fetched, window, offsets, factor, t):
            nc.scalar.activation(
                out=fetched, in_=window[:].indirect(offsets[:]), func=COPY, scale=factor[:, t : t + 1]
            )

        def weave(planes, name, tag=None):
            woven = sbuf([P, planes.shape[2], PACK], BF16, name, tag=tag)
            nc.vector.tensor_copy(
                out=woven[:].rearrange("p (c i) t -> p c t i", i=4),
                in_=planes.rearrange("p t (c i) -> p c t i", i=4),
            )
            return woven

        def quantise(woven_halves, name):
            half = woven_halves[0].shape[1]
            codes = sbuf([P, 2 * half], U32, name + "_codes")
            plane = sbuf([P, 2 * half], U8, name + "_plane")
            for h, woven in enumerate(woven_halves):
                nc.vector.quantize_mx(
                    out=codes[:, half * h : half * (h + 1)].bitcast(E4M3),
                    scales=plane[:, half * h : half * (h + 1)],
                    in_=woven[:].rearrange("p c t -> p (c t)"),
                )
            return codes, plane

        xo_plane_table = sbuf([P, M], U8, "xo_plane_table")
        nc.vector.memset(xo_plane_table[:].bitcast(I32), 0)

        w_staged = stage_scale_rows(nc.scalar, w_scales, "w_staged")
        ga_sb = load_column(nc.scalar, ga, "ga_sb")
        gb_sb = load_column(nc.scalar, gb, "gb_sb")
        w2_staged = stage_scale_rows(nc.scalar, w2_scales, "w2_staged")

        offs_sb = load_list(offs, "offs_sb")
        offs2_sb = load_list(offs2, "offs2_sb")
        ta_sb, tb_sb = [], []
        for t in range(PACK):
            ta_sb.append(load_rows(ta, t, "ta%d" % t))
            tb_sb.append(load_rows(tb, t, "tb%d" % t))
        w_raw = sbuf([P, 2 * R], U8, "w_raw")
        nc.sync.dma_start(out=w_raw[:].bitcast(I32), in_=w_words[0].bitcast(I32))
        offs3_sb = load_list(offs3, "offs3_sb")
        xo_table = sbuf([P, M], U16, "xo_table")
        nc.sync.dma_start(out=xo_table[:].bitcast(I32), in_=xo_words[0].bitcast(I32))
        xo_rows = xo_scales[0].bitcast(I32).rearrange("(q i) c -> i q c", i=PACK)
        for i in range(PACK):
            nc.sync.dma_start(out=xo_plane_table[i:P:32, :].bitcast(I32), in_=xo_rows[i])
        offs4_sb = load_list(offs4, "offs4_sb")
        w2_raw = sbuf([P, R], U32, "w2_raw")
        nc.sync.dma_start(out=w2_raw[:].bitcast(I32), in_=w2_words[0].rearrange("p c t -> p (c t)").bitcast(I32))
        ea_sb = load_column(nc.sync, ea, "ea_sb")
        va_sb = [load_rows(va, 0, "va0")]
        offs7_sb = load_list(offs7, "offs7_sb")
        offs5_sb = load_list(offs5, "offs5_sb")
        sa_sb = load_column(nc.sync, sa, "sa_sb")
        va_sb.append(load_rows(va, 1, "va1"))
        va_sb.append(load_rows(va, 2, "va2"))
        va_sb.append(load_rows(va, 3, "va3"))
        offs6_sb = load_list(offs6, "offs6_sb")
        sb_sb = load_column(nc.sync, sb, "sb_sb")

        w_plane_raw = spread_scale_rows(w_staged, "w_plane_raw")
        w2_plane_raw = spread_scale_rows(w2_staged, "w2_plane_raw")

        boards = [sbuf([P, C], F32, "board%d" % t) for t in range(PACK)]
        for board in boards:
            nc.vector.memset(board[:], 0.0)

        w_plane = sbuf([P, R], U8, "w_plane")
        deal_columns(nc.vector.tensor_copy, w_plane[:], w_plane_raw[:])
        w2_plane = sbuf([P, R], U8, "w2_plane")
        deal_columns(nc.vector.tensor_copy, w2_plane[:], w2_plane_raw[:])

        xc_woven = [sbuf([P, J // 2, PACK], BF16, "xc_woven%d" % h) for h in range(2)]
        for t in range(PACK):
            from_ta = sbuf([P, J], F32, "from_ta%d" % t)
            fetch_scaled(from_ta[:], ta_sb[t], offs_sb, ga_sb, t)
            from_tb = sbuf([P, J], F32, "from_tb%d" % t)
            fetch_scaled(from_tb[:], tb_sb[t], offs2_sb, gb_sb, t)
            for h in range(2):
                slots = slice(h * J // 2, (h + 1) * J // 2)
                nc.vector.tensor_tensor(out=xc_woven[h][:, :, t], in0=from_ta[:, slots], in1=from_tb[:, slots], op=ADD)
        xc_codes, xc_plane = quantise(xc_woven, "xc")

        w_dealt = sbuf([P, 2 * R], U8, "w_dealt")
        deal_columns(nc.scalar.copy, w_dealt[:].bitcast(U16), w_raw[:].bitcast(U16))

        a_sb = []
        for t in range(PACK):
            a_ps = psum.tile([P, J], F32, name="a_ps%d" % t)
            nc.tensor.matmul_mx(
                out=a_ps[:],
                lhsT=w_dealt[:, 2 * P * t : 2 * P * (t + 1)].bitcast(E2M1),
                lhsT_scale=w_plane[:, P * t : P * (t + 1)],
                rhs=xc_codes[:].bitcast(E4M3),
                rhs_scale=xc_plane[:],
                start=True,
                stop=True,
            )
            a_sb.append(sbuf([P, J], F32, "a_sb%d" % t))
            nc.scalar.copy(out=a_sb[t][:], in_=a_ps[:])

        w2_dealt = sbuf([P, R], U32, "w2_dealt")
        deal_columns(nc.scalar.copy, w2_dealt[:], w2_raw[:])
        xo_codes = sbuf([P, J], U16, "xo_codes")
        nc.vector.tensor_copy(out=xo_codes[:], in_=xo_table[:].indirect(offs3_sb[:]))
        xo_plane = sbuf([P, J], U8, "xo_plane")
        nc.vector.tensor_copy(out=xo_plane[:], in_=xo_plane_table[:].indirect(offs3_sb[:]))
        b_ps = [psum.tile([P, 2, J], F32, name="b_ps%d" % u) for u in range(2)]
        for t in range(PACK):
            nc.tensor.matmul_mx(
                out=b_ps[t // 2][:, t % 2, :],
                lhsT=w2_dealt[:, P * t : P * (t + 1)].bitcast(E4M3),
                lhsT_scale=w2_plane[:, P * t : P * (t + 1)],
                rhs=xo_codes[:].bitcast(E2M1),
                rhs_scale=xo_plane[:],
                start=True,
                stop=True,
            )

        for t in range(PACK):
            nc.vector.tensor_copy(out=boards[t][:].indirect(offs4_sb[:]), in_=a_sb[t][:])

        vc_planes = sbuf([P, PACK, N], BF16, "vc_planes")
        for t in range(PACK):
            fetch_scaled(vc_planes[:, t, :], va_sb[t], offs7_sb, ea_sb, t)

        g1 = []
        for t in range(PACK):
            read_back = sbuf([P, J], F32, "read_back%d" % t, tag="va%d" % t)
            fetch_scaled(read_back[:], boards[t], offs5_sb, sa_sb, t)
            g1.append(sbuf([P, J], F32, "g1_%d" % t))
            nc.vector.tensor_tensor(out=g1[t][:], in0=read_back[:], in1=b_ps[t // 2][:, t % 2, :], op=MAX)
        vc_woven = [
            weave(vc_planes[:, :, h * N // 2 : (h + 1) * N // 2], "vc_woven%d" % h, tag="va%d" % (2 + h))
            for h in range(2)
        ]
        vc_codes, vc_plane = quantise(vc_woven, "vc")
        hid_planes = sbuf([P, PACK, O], BF16, "hid_planes", tag="board3")
        for t in range(PACK):
            fetch_scaled(hid_planes[:, t, :], g1[t], offs6_sb, sb_sb, t)
        hid_woven = [
            weave(hid_planes[:, :, h * O // 2 : (h + 1) * O // 2], "hid_woven%d" % h)
            for h in range(2)
        ]
        hid_codes, hid_plane = quantise(hid_woven, "hid")

        for u, (copy, queue) in enumerate(((nc.vector.tensor_copy, nc.sync), (nc.scalar.copy, nc.scalar))):
            y_ps = psum.tile([P, O], F32, name="y_ps%d" % u)
            nc.tensor.matmul_mx(
                out=y_ps[:],
                lhsT=vc_codes[:, P * u : P * (u + 1)].bitcast(E4M3),
                lhsT_scale=vc_plane[:, P * u : P * (u + 1)],
                rhs=hid_codes[:].bitcast(E4M3),
                rhs_scale=hid_plane[:],
                start=True,
                stop=True,
            )
            y_sb = sbuf([P, O], F32, "y_sb%d" % u)
            copy(out=y_sb[:], in_=y_ps[:])
            queue.dma_start(out=out[P * u : P * (u + 1), :], in_=y_sb[:])
